import numpy as np
import ml_dtypes


def mxq(x, axis, fmt="e4m3"):
    dtype, down = {"e4m3": (ml_dtypes.float8_e4m3fn, 7), "e5m2": (ml_dtypes.float8_e5m2, 14)}[fmt]
    v = np.moveaxis(np.asarray(x, np.float32).astype(ml_dtypes.bfloat16).astype(np.float64), axis, -1)
    blocks = v.reshape(v.shape[:-1] + (-1, 32))
    amax = np.abs(blocks).max(-1, keepdims=True)
    byte = np.maximum(np.where(amax > 0, np.frexp(amax)[1] - 1 + 127, 0) - down, 1)
    scale = np.exp2(byte - 127.0)
    codes = (blocks / scale).astype(np.float32).astype(dtype).astype(np.float64)
    return np.moveaxis((codes * scale).reshape(v.shape), -1, axis)


WIDE = False


def mx_kscale(k):
    if not WIDE:
        return np.ones(k)
    levels = np.array([10, -10, 5, -5, 0])
    if k % 512:
        return np.exp2(np.random.permutation(np.resize(levels, k // 32))).repeat(32)
    a = np.empty((k // 512, 16))
    for p in range(k // 512):
        a[p, :8] = np.random.permutation(np.resize(levels, 8))
        for g in range(8):
            far = levels[np.abs(levels - a[p, g]) >= 10]
            a[p, g + 8] = far[np.random.randint(len(far))]
    return np.exp2(a.ravel()).repeat(32)


def f64(x):
    return np.asarray(x).astype(np.float64)


def striped(idx):
    return np.tile(idx.reshape(-1, 16).T, (8, 1)).astype(np.uint16)


def unstriped(offs):
    return offs[:16].T.reshape(-1).astype(np.int64)


def gelu(v):
    return 0.5 * v * (1.0 + np.tanh(np.sqrt(2.0 / np.pi) * (v + 0.044715 * v**3)))


K, T, S, V, H, N = 1024, 1024, 512, 1024, 1024, 512
P = 2 ** 7


def setup_inputs():
    n = np.random.standard_normal
    s = mx_kscale(K)[:, None]
    u = mx_kscale(H)
    return {
        "xT": (n((K, T)) * s).astype(np.float32),
        "w1": (n((K, H)) / np.sqrt(K) / s * u).astype(np.float32),
        "w2": (n((H, N)) / np.sqrt(H) / u[:, None]).astype(np.float32),
        "gate": np.tile(np.random.uniform(0.5, 1.5, S), (P, 1)).astype(np.float32),
        "offs": striped(np.random.permutation(T)[:S]),
        "pos1": striped(np.random.permutation(V)[:S]),
    }


def reference(xT, w1, w2, gate, offs, pos1):
    h = gelu(mxq(f64(w1), 0, "e4m3").T @ mxq(f64(xT)[:, unstriped(offs)], 0, "e4m3"))
    z = np.zeros((H, V))
    z[:, unstriped(pos1)] = f64(gate)[:1] * h
    return mxq(f64(w2), 0, "e4m3").T @ mxq(z, 0, "e4m3")

@@ -1,0 +1,263 @@
+from contextlib import ExitStack
+
+import concourse.mybir as mybir
+
+K, T, S, V, H, N = 1024, 1024, 512, 1024, 1024, 512
+
+F32 = mybir.dt.float32
+BF16 = mybir.dt.bfloat16
+U32 = mybir.dt.uint32
+U16 = mybir.dt.uint16
+U8 = mybir.dt.uint8
+FP8X4 = mybir.dt.float8_e4m3fn_x4
+
+MULT = mybir.AluOpType.mult
+GELU = mybir.ActivationFunctionType.Gelu_apprx_tanh
+
+P = 128
+PACK = 4
+K_PASS = P * PACK
+PASSES = 2
+COLS = 512
+
+FLOPS = 2 * K * S * H + 2 * H * V * N
+
+
+def tile_picked_voxel_gelu_e_kernel(tc, xT, w1, w2, gate, offs, pos1, out):
+    nc = tc.nc
+    with ExitStack() as ctx:
+        lists = ctx.enter_context(tc.tile_pool(name="lists", bufs=1))
+        keep = ctx.enter_context(tc.tile_pool(name="keep", bufs=1))
+        ring = ctx.enter_context(tc.tile_pool(name="ring", bufs=5))
+        psum = ctx.enter_context(tc.psum_pool(name="psum", bufs=8))
+
+        idx = lists.tile([P, S // 16], U16, name="idx")
+        cell = lists.tile([P, S // 16], U16, name="cell")
+        nc.sync.dma_start(idx[:], offs)
+
+        x_planes = {}
+
+        def load_rows(source, name):
+            raw = keep.tile([P, PACK, COLS], F32, name=name)
+            nc.sync.dma_start(out=raw[:], in_=source.rearrange("(p j) c -> p j c", j=PACK))
+            return raw
+
+        w1_raw = {}
+        w2_raw = {}
+        for s in range(PASSES):
+            rows = xT[s * K_PASS : (s + 1) * K_PASS, :].rearrange("(p t) c -> p t c", t=PACK)
+            for t in range(PACK):
+                plane = keep.tile([P, T], F32, name=f"x_{s}_{t}")
+                nc.sync.dma_start(out=plane[:], in_=rows[:, t, :])
+                x_planes[s, t] = plane
+            w1_raw[0, s] = load_rows(w1[s * K_PASS : (s + 1) * K_PASS, 0:COLS], f"w1_raw_0_{s}")
+        nc.sync.dma_start(cell[:], pos1)
+        gate_all = keep.tile([P, S], F32, name="gate_all")
+        nc.sync.dma_start(out=gate_all[:], in_=gate)
+        for s in range(PASSES):
+            w1_raw[1, s] = load_rows(w1[s * K_PASS : (s + 1) * K_PASS, COLS : 2 * COLS], f"w1_raw_1_{s}")
+        for g in range(PASSES):
+            w2_raw[g] = load_rows(w2[g * K_PASS : (g + 1) * K_PASS, :], f"w2_raw_{g}")
+
+        warm = keep.tile([P, 2], F32, name="warm")
+        nc.gpsimd.memset(warm[:], 0.0)
+        warmed = keep.tile([P, 2], F32, name="warmed")
+        nc.scalar.activation(out=warmed[:], in_=warm[:], func=GELU)
+
+        z_all = []
+        for g in range(PASSES):
+            z_group = keep.tile([P, PACK * V], BF16, name=f"z_all_{g}", align_bytes=64)
+            z_all.append(z_group)
+        z_plane = {}
+        for t in range(PACK):
+            plane = keep.tile([P, V], F32, name=f"z_plane_{t}")
+            nc.gpsimd.memset(plane[:], 0.0)
+            z_plane[t] = plane
+
+        def new_operand(cols, name):
+            codes = keep.tile([P, cols], U32, name=name + "_codes", align_bytes=64)
+            scales = keep.tile([P, cols], U8, name=name + "_scales", align_bytes=64)
+            return codes, scales
+
+        def quantize(operand, c0, grouped, g0, width):
+            codes, scales = operand
+            nc.vector.quantize_mx(
+                out=codes[:, c0 : c0 + width].bitcast(FP8X4),
+                scales=scales[:, c0 : c0 + width],
+                in_=grouped[:, PACK * g0 : PACK * (g0 + width)],
+            )
+
+        def new_grouped():
+            return ring.tile([P, PACK * COLS], BF16, name="grouped", align_bytes=64)
+
+        def quad_view(grouped_cols):
+            return grouped_cols.rearrange("p (c i t) -> p c t i", i=4, t=PACK)
+
+        def quad_read(source):
+            return source.rearrange("p t (c i) -> p c t i", i=4)
+
+        x_q = []
+        w1_q = {}
+        w1_grouped = {}
+
+        def w1_view(grouped, m0, m1):
+            return grouped[:].rearrange("p (t m j) -> p m t j", t=PACK, j=PACK)[:, m0:m1]
+
+        def w1_read(raw, m0, m1):
+            return raw[:].rearrange("p j (m t) -> p m t j", t=PACK)[:, m0:m1]
+
+        def cast_w1(g, s, split):
+            grouped = new_grouped()
+            if split:
+                nc.vector.tensor_copy(out=w1_view(grouped, 0, split), in_=w1_read(w1_raw[g, s], 0, split))
+            nc.scalar.copy(out=w1_view(grouped, split, P), in_=w1_read(w1_raw[g, s], split, P))
+            w1_grouped[g, s] = grouped
+
+        def quantize_w1(g, s, pieces):
+            w1_q[g, s] = new_operand(COLS, f"w1_{g}_{s}")
+            width = COLS // pieces
+            for i in range(pieces):
+                quantize(w1_q[g, s], i * width, w1_grouped[g, s], i * width, width)
+
+        for s in range(PASSES):
+            picked = keep.tile([P, PACK, S], F32, name=f"picked_{s}")
+            for t in range(PACK):
+                nc.vector.tensor_copy(picked[:, t, :], x_planes[s, t][:].indirect(idx[:]))
+            grouped = new_grouped()
+            cut = 0 if s == 0 else 320
+            if cut:
+                nc.vector.tensor_copy(out=quad_view(grouped[:, : PACK * cut]), in_=quad_read(picked[:, :, :cut]))
+            nc.scalar.copy(out=quad_view(grouped[:, PACK * cut :]), in_=quad_read(picked[:, :, cut:]))
+            operand = new_operand(S, f"x_{s}")
+            quantize(operand, 0, grouped, 0, S)
+            x_q.append(operand)
+            cast_w1(0, s, 64 * s)
+            quantize_w1(0, s, 1 if s == 0 else PACK)
+
+        hidden = {}
+
+        def layer1(g, t):
+            acc = psum.tile([P, S], F32, name="acc")
+            cols = slice(t * P, (t + 1) * P)
+            for s in range(PASSES):
+                w_codes, w_scales = w1_q[g, s]
+                x_codes, x_scales = x_q[s]
+                nc.tensor.matmul_mx(
+                    out=acc[:],
+                    lhsT=w_codes[:, cols].bitcast(FP8X4),
+                    lhsT_scale=w_scales[:, cols],
+                    rhs=x_codes[:].bitcast(FP8X4),
+                    rhs_scale=x_scales[:],
+                    start=(s == 0),
+                    stop=(s == PASSES - 1),
+                )
+            h = ring.tile([P, S], F32, name="h")
+            nc.scalar.activation(out=h[:], in_=acc[:], func=GELU)
+            gated = ring.tile([P, S], F32, name="gated")
+            nc.gpsimd.tensor_tensor(gated[:], h[:], gate_all[:], MULT)
+            hidden[g, t] = gated
+
+        def scatter(g, t):
+            nc.vector.tensor_copy(z_plane[t][:].indirect(cell[:]), hidden[g, t][:])
+
+        def collect(g, t):
+            nc.scalar.copy(out=z_all[g][:, t * V : (t + 1) * V], in_=z_plane[t][:])
+
+        w2_q = []
+        w2_grouped = []
+
+        def cast_w2(g):
+            grouped = new_grouped()
+            nc.scalar.copy(out=quad_view(grouped[:]), in_=quad_read(w2_raw[g][:]))
+            w2_grouped.append(grouped)
+
+        def quantize_w2(g):
+            operand = new_operand(N, f"w2_{g}")
+            quantize(operand, 0, w2_grouped[g], 0, N)
+            w2_q.append(operand)
+
+        z_q = [new_operand(V, f"z_{g}") for g in range(PASSES)]
+
+        def z_read(g, v0, v1):
+            return quad_read(z_all[g][:].rearrange("p (t v) -> p t v", t=PACK)[:, :, v0:v1])
+
+        accs = {}
+
+        def layer2(g, n):
+            z_codes, z_scales = z_q[g]
+            w_codes, w_scales = w2_q[g]
+            cols = slice(n * COLS, (n + 1) * COLS)
+            for m in range(N // P):
+                if g == 0:
+                    acc = psum.tile([P, COLS], F32, name="acc")
+                    accs[m, n] = acc
+                rows = slice(m * P, (m + 1) * P)
+                nc.tensor.matmul_mx(
+                    out=accs[m, n][:],
+                    lhsT=w_codes[:, rows].bitcast(FP8X4),
+                    lhsT_scale=w_scales[:, rows],
+                    rhs=z_codes[:, cols].bitcast(FP8X4),
+                    rhs_scale=z_scales[:, cols],
+                    start=(g == 0),
+                    stop=(g == PASSES - 1),
+                )
+
+        def store(n):
+            for m in range(N // P):
+                result = keep.tile([P, COLS], F32, name=f"result_{m}_{n}")
+                if m % 2 == 0:
+                    nc.vector.tensor_copy(out=result[:], in_=accs[m, n][:])
+                else:
+                    nc.scalar.copy(out=result[:], in_=accs[m, n][:])
+                nc.sync.dma_start(out=out[m * P : (m + 1) * P, n * COLS : (n + 1) * COLS], in_=result[:])
+
+        for t in range(PACK):
+            layer1(0, t)
+        scatter(0, 0)
+        collect(0, 0)
+        cast_w1(1, 0, 0)
+        quantize_w1(1, 0, 1)
+        scatter(0, 1)
+        cast_w1(1, 1, 0)
+        collect(0, 1)
+        quantize_w1(1, 1, 1)
+        scatter(0, 2)
+        layer1(1, 1)
+        collect(0, 2)
+        cast_w2(0)
+        layer1(1, 2)
+        scatter(0, 3)
+        quantize_w2(0)
+        collect(0, 3)
+        layer1(1, 3)
+        scatter(1, 1)
+        collect(1, 1)
+        z_grouped = []
+        for n in range(2):
+            grouped = new_grouped()
+            nc.scalar.copy(out=quad_view(grouped[:]), in_=z_read(0, n * COLS, (n + 1) * COLS))
+            z_grouped.append(grouped)
+        scatter(1, 2)
+        collect(1, 2)
+        layer1(1, 0)
+        cast_w2(1)
+        scatter(1, 3)
+        collect(1, 3)
+        quantize_w2(1)
+        for n in range(2):
+            quantize(z_q[0], n * COLS, z_grouped[n], 0, COLS)
+            layer2(0, n)
+        scatter(1, 0)
+        for v0 in (0, COLS):
+            nc.vector.tensor_copy(out=z_all[1][:, v0 : v0 + COLS], in_=z_plane[0][:, v0 : v0 + COLS])
+
+        near = new_grouped()
+        far = new_grouped()
+        nc.vector.tensor_copy(out=quad_view(near[:]), in_=z_read(1, 0, COLS))
+        nc.scalar.copy(out=quad_view(far[:]), in_=z_read(1, COLS, V))
+        quantize(z_q[1], 0, near, 0, COLS)
+        layer2(1, 0)
+        quantize(z_q[1], COLS, far, 0, COLS)
+        layer2(1, 1)
+        store(0)
+        store(1)

@@ -20,6 +20,8 @@ K_PASS = P * PACK
 PASSES = 2
 COLS = 512
 
+X_CUT = (320, 320, 192, 256)
+
 FLOPS = 2 * K * S * H + 2 * H * V * N
 
 
@@ -35,41 +37,51 @@ def tile_picked_voxel_gelu_e_kernel(tc, xT, w1, w2, gate, offs, pos1, out):
         cell = lists.tile([P, S // 16], U16, name="cell")
         nc.sync.dma_start(idx[:], offs)
 
-        x_planes = {}
-
         def load_rows(source, name):
             raw = keep.tile([P, PACK, COLS], F32, name=name)
             nc.sync.dma_start(out=raw[:], in_=source.rearrange("(p j) c -> p j c", j=PACK))
             return raw
 
-        w1_raw = {}
-        w2_raw = {}
+        def rows(k):
+            return slice(k * K_PASS, (k + 1) * K_PASS)
+
+        x_raw = {}
         for s in range(PASSES):
-            rows = xT[s * K_PASS : (s + 1) * K_PASS, :].rearrange("(p t) c -> p t c", t=PACK)
-            for t in range(PACK):
-                plane = keep.tile([P, T], F32, name=f"x_{s}_{t}")
-                nc.sync.dma_start(out=plane[:], in_=rows[:, t, :])
-                x_planes[s, t] = plane
-            w1_raw[0, s] = load_rows(w1[s * K_PASS : (s + 1) * K_PASS, 0:COLS], f"w1_raw_0_{s}")
+            for c in range(2):
+                x_raw[s, c] = load_rows(xT[rows(s), c * COLS : (c + 1) * COLS], f"x_raw_{s}_{c}")
+        w1_raw = {}
+        for s in range(PASSES):
+            w1_raw[0, s] = load_rows(w1[rows(s), 0:COLS], f"w1_raw_0_{s}")
         nc.sync.dma_start(cell[:], pos1)
         gate_all = keep.tile([P, S], F32, name="gate_all")
         nc.sync.dma_start(out=gate_all[:], in_=gate)
         for s in range(PASSES):
-            w1_raw[1, s] = load_rows(w1[s * K_PASS : (s + 1) * K_PASS, COLS : 2 * COLS], f"w1_raw_1_{s}")
+            w1_raw[1, s] = load_rows(w1[rows(s), COLS : 2 * COLS], f"w1_raw_1_{s}")
+        w2_raw = []
         for g in range(PASSES):
-            w2_raw[g] = load_rows(w2[g * K_PASS : (g + 1) * K_PASS, :], f"w2_raw_{g}")
+            w2_raw.append(load_rows(w2[rows(g), :], f"w2_raw_{g}"))
 
         warm = keep.tile([P, 2], F32, name="warm")
         nc.gpsimd.memset(warm[:], 0.0)
         warmed = keep.tile([P, 2], F32, name="warmed")
         nc.scalar.activation(out=warmed[:], in_=warm[:], func=GELU)
+        first_bias = keep.tile([P, 1], F32, name="first_bias", tag="after_first_gelu", align_bytes=64)
+        nc.gpsimd.memset(first_bias[:], 0.0)
+
+        all_bytes = keep.tile([P, T], U8, name="x_all_bytes", align_bytes=64)
+        nc.gpsimd.memset(all_bytes[:], 0)
+        x_all = []
+        for s in range(PASSES):
+            words = keep.tile([P, T], U32, name=f"x_all_words_{s}", align_bytes=64)
+            x_all.append((words, all_bytes[4 * s : P, :]))
 
         z_all = []
         for g in range(PASSES):
-            z_group = keep.tile([P, PACK * V], BF16, name=f"z_all_{g}", align_bytes=64)
+            z_group = keep.tile([P, PACK * V], F32, name=f"z_all_{g}")
+            nc.gpsimd.memset(z_group[:, 0:V], 0.0)
             z_all.append(z_group)
         z_plane = {}
-        for t in range(PACK):
+        for t in range(1, PACK):
             plane = keep.tile([P, V], F32, name=f"z_plane_{t}")
             nc.gpsimd.memset(plane[:], 0.0)
             z_plane[t] = plane
@@ -87,8 +99,8 @@ def tile_picked_voxel_gelu_e_kernel(tc, xT, w1, w2, gate, offs, pos1, out):
                 in_=grouped[:, PACK * g0 : PACK * (g0 + width)],
             )
 
-        def new_grouped():
-            return ring.tile([P, PACK * COLS], BF16, name="grouped", align_bytes=64)
+        def new_grouped(cols, slot):
+            return keep.tile([P, PACK * cols], BF16, name="grouped", tag=slot, align_bytes=64)
 
         def quad_view(grouped_cols):
             return grouped_cols.rearrange("p (c i t) -> p c t i", i=4, t=PACK)
@@ -96,43 +108,52 @@ def tile_picked_voxel_gelu_e_kernel(tc, xT, w1, w2, gate, offs, pos1, out):
         def quad_read(source):
             return source.rearrange("p t (c i) -> p c t i", i=4)
 
-        x_q = []
+        def cast_part(engine_copy, grouped, source, c0, c1):
+            engine_copy(out=quad_view(grouped[:, PACK * c0 : PACK * c1]), in_=quad_read(source[:, :, c0:c1]))
+
         w1_q = {}
         w1_grouped = {}
 
-        def w1_view(grouped, m0, m1):
-            return grouped[:].rearrange("p (t m j) -> p m t j", t=PACK, j=PACK)[:, m0:m1]
+        def cast_w1(engine_copy, g, s, t0, t1):
+            if (g, s) not in w1_q:
+                w1_q[g, s] = new_operand(COLS, f"w1_{g}_{s}")
+            if (g, s) == (0, 1):
+                base, planes, slot = (0, 2, "w_01") if t0 < 2 else (2, 2, "after_first_gelu")
+            else:
+                base, planes, slot = 0, PACK, "w_b" if (g, s) == (1, 0) else "w_a"
+            if (g, s, base) not in w1_grouped:
+                grouped = new_grouped(planes * P, slot)
+                w1_grouped[g, s, base] = grouped
+            view = w1_grouped[g, s, base][:].rearrange("p (t m j) -> p m t j", t=planes, j=PACK)
+            read = w1_raw[g, s][:].rearrange("p j (m t) -> p m t j", t=PACK)
+            engine_copy(out=view[:, :, t0 - base : t1 - base], in_=read[:, :, t0:t1])
 
-        def w1_read(raw, m0, m1):
-            return raw[:].rearrange("p j (m t) -> p m t j", t=PACK)[:, m0:m1]
+        def quantize_w1(g, s, t0, t1):
+            base = 2 if (g, s) == (0, 1) and t0 >= 2 else 0
+            quantize(w1_q[g, s], t0 * P, w1_grouped[g, s, base], (t0 - base) * P, (t1 - t0) * P)
 
-        def cast_w1(g, s, split):
-            grouped = new_grouped()
-            if split:
-                nc.vector.tensor_copy(out=w1_view(grouped, 0, split), in_=w1_read(w1_raw[g, s], 0, split))
-            nc.scalar.copy(out=w1_view(grouped, split, P), in_=w1_read(w1_raw[g, s], split, P))
-            w1_grouped[g, s] = grouped
-
-        def quantize_w1(g, s, pieces):
-            w1_q[g, s] = new_operand(COLS, f"w1_{g}_{s}")
-            width = COLS // pieces
-            for i in range(pieces):
-                quantize(w1_q[g, s], i * width, w1_grouped[g, s], i * width, width)
-
+        x_words = []
+        x_bytes = []
         for s in range(PASSES):
-            picked = keep.tile([P, PACK, S], F32, name=f"picked_{s}")
-            for t in range(PACK):
-                nc.vector.tensor_copy(picked[:, t, :], x_planes[s, t][:].indirect(idx[:]))
-            grouped = new_grouped()
-            cut = 0 if s == 0 else 320
-            if cut:
-                nc.vector.tensor_copy(out=quad_view(grouped[:, : PACK * cut]), in_=quad_read(picked[:, :, :cut]))
-            nc.scalar.copy(out=quad_view(grouped[:, PACK * cut :]), in_=quad_read(picked[:, :, cut:]))
-            operand = new_operand(S, f"x_{s}")
-            quantize(operand, 0, grouped, 0, S)
-            x_q.append(operand)
-            cast_w1(0, s, 64 * s)
-            quantize_w1(0, s, 1 if s == 0 else PACK)
+            for c in range(2):
+                grouped = new_grouped(COLS, "x_a" if c == 0 else "x_b")
+                cut = X_CUT[2 * s + c]
+                if cut:
+                    cast_part(nc.vector.tensor_copy, grouped, x_raw[s, c], 0, cut)
+                cast_part(nc.scalar.copy, grouped, x_raw[s, c], cut, COLS)
+                quantize(x_all[s], c * COLS, grouped, 0, COLS)
+            words = keep.tile([P, S], U32, name=f"x_words_{s}", align_bytes=64)
+            nc.vector.tensor_copy(words[:], x_all[s][0][:].indirect(idx[:]))
+            x_words.append(words)
+        picked_bytes = keep.tile([P, S], U8, name="x_bytes", align_bytes=64)
+        nc.vector.tensor_copy(picked_bytes[:], all_bytes[:].indirect(idx[:]))
+        x_bytes = [picked_bytes[4 * s : P, :] for s in range(PASSES)]
+
+        cast_w1(nc.scalar.copy, 0, 0, 0, PACK)
+        cast_w1(nc.scalar.copy, 0, 1, 0, 1)
+        cast_w1(nc.scalar.copy, 0, 1, 1, 2)
+        quantize_w1(0, 0, 0, PACK)
+        quantize_w1(0, 1, 0, 1)
 
         hidden = {}
 
@@ -141,61 +162,57 @@ def tile_picked_voxel_gelu_e_kernel(tc, xT, w1, w2, gate, offs, pos1, out):
             cols = slice(t * P, (t + 1) * P)
             for s in range(PASSES):
                 w_codes, w_scales = w1_q[g, s]
-                x_codes, x_scales = x_q[s]
                 nc.tensor.matmul_mx(
                     out=acc[:],
                     lhsT=w_codes[:, cols].bitcast(FP8X4),
                     lhsT_scale=w_scales[:, cols],
-                    rhs=x_codes[:].bitcast(FP8X4),
-                    rhs_scale=x_scales[:],
+                    rhs=x_words[s][:].bitcast(FP8X4),
+                    rhs_scale=x_bytes[s],
                     start=(s == 0),
                     stop=(s == PASSES - 1),
                 )
-            h = ring.tile([P, S], F32, name="h")
-            nc.scalar.activation(out=h[:], in_=acc[:], func=GELU)
-            gated = ring.tile([P, S], F32, name="gated")
-            nc.gpsimd.tensor_tensor(gated[:], h[:], gate_all[:], MULT)
-            hidden[g, t] = gated
+            if (g, t) == (1, 0):
+                h = keep.tile([P, S], F32, name="h_last", tag="z_all_0")
+            else:
+                h = ring.tile([P, S], F32, name="h")
+            if (g, t) == (0, 0):
+                nc.scalar.activation(out=h[:], in_=acc[:], func=GELU, bias=first_bias[:])
+            else:
+                nc.scalar.activation(out=h[:], in_=acc[:], func=GELU)
+            hidden[g, t] = h
 
         def scatter(g, t):
-            nc.vector.tensor_copy(z_plane[t][:].indirect(cell[:]), hidden[g, t][:])
+            window = z_all[g] if t == 0 else z_plane[t]
+            nc.vector.tensor_tensor(window[:].indirect(cell[:]), hidden[g, t][:], gate_all[:], MULT)
 
-        def collect(g, t):
-            nc.scalar.copy(out=z_all[g][:, t * V : (t + 1) * V], in_=z_plane[t][:])
+        def collect(g, t, last):
+            region = z_all[g][:, t * V : (t + 1) * V]
+            if last:
+                nc.scalar.copy(out=region, in_=z_plane[t][:])
+            else:
+                nc.sync.dma_start(out=region, in_=z_plane[t][:])
 
-        w2_q = []
-        w2_grouped = []
-
-        def cast_w2(g):
-            grouped = new_grouped()
-            nc.scalar.copy(out=quad_view(grouped[:]), in_=quad_read(w2_raw[g][:]))
-            w2_grouped.append(grouped)
-
-        def quantize_w2(g):
-            operand = new_operand(N, f"w2_{g}")
-            quantize(operand, 0, w2_grouped[g], 0, N)
-            w2_q.append(operand)
-
+        w2_q = new_operand(PASSES * N, "w2")
         z_q = [new_operand(V, f"z_{g}") for g in range(PASSES)]
 
-        def z_read(g, v0, v1):
-            return quad_read(z_all[g][:].rearrange("p (t v) -> p t v", t=PACK)[:, :, v0:v1])
+        def z_read(g):
+            return z_all[g][:].rearrange("p (t v) -> p t v", t=PACK)
 
         accs = {}
 
         def layer2(g, n):
             z_codes, z_scales = z_q[g]
-            w_codes, w_scales = w2_q[g]
+            w_codes, w_scales = w2_q
             cols = slice(n * COLS, (n + 1) * COLS)
             for m in range(N // P):
                 if g == 0:
                     acc = psum.tile([P, COLS], F32, name="acc")
                     accs[m, n] = acc
-                rows = slice(m * P, (m + 1) * P)
+                weights = slice(g * N + m * P, g * N + (m + 1) * P)
                 nc.tensor.matmul_mx(
                     out=accs[m, n][:],
-                    lhsT=w_codes[:, rows].bitcast(FP8X4),
-                    lhsT_scale=w_scales[:, rows],
+                    lhsT=w_codes[:, weights].bitcast(FP8X4),
+                    lhsT_scale=w_scales[:, weights],
                     rhs=z_codes[:, cols].bitcast(FP8X4),
                     rhs_scale=z_scales[:, cols],
                     start=(g == 0),
@@ -211,52 +228,57 @@ def tile_picked_voxel_gelu_e_kernel(tc, xT, w1, w2, gate, offs, pos1, out):
                     nc.scalar.copy(out=result[:], in_=accs[m, n][:])
                 nc.sync.dma_start(out=out[m * P : (m + 1) * P, n * COLS : (n + 1) * COLS], in_=result[:])
 
-        for t in range(PACK):
-            layer1(0, t)
+        layer1(0, 0)
+        quantize_w1(0, 1, 1, 2)
         scatter(0, 0)
-        collect(0, 0)
-        cast_w1(1, 0, 0)
-        quantize_w1(1, 0, 1)
+        cast_w1(nc.scalar.copy, 0, 1, 2, PACK)
+        quantize_w1(0, 1, 2, PACK)
+        layer1(0, 1)
         scatter(0, 1)
-        cast_w1(1, 1, 0)
-        collect(0, 1)
-        quantize_w1(1, 1, 1)
+        cast_w1(nc.scalar.copy, 1, 0, 0, PACK)
+        quantize_w1(1, 0, 0, PACK)
+        cast_w1(nc.scalar.copy, 1, 1, 0, PACK)
+        quantize_w1(1, 1, 0, PACK)
+        layer1(0, 2)
         scatter(0, 2)
-        layer1(1, 1)
-        collect(0, 2)
-        cast_w2(0)
-        layer1(1, 2)
+        collect(0, 1, False)
+        layer1(0, 3)
         scatter(0, 3)
-        quantize_w2(0)
-        collect(0, 3)
-        layer1(1, 3)
+        collect(0, 2, False)
+        layer1(1, 1)
+        w2_grouped = new_grouped(PASSES * N, "w2_grouped")
+        for g in range(PASSES):
+            nc.scalar.copy(
+                out=quad_view(w2_grouped[:, g * PACK * N : (g + 1) * PACK * N]), in_=quad_read(w2_raw[g][:])
+            )
+        quantize(w2_q, 0, w2_grouped, 0, PASSES * N)
         scatter(1, 1)
-        collect(1, 1)
-        z_grouped = []
-        for n in range(2):
-            grouped = new_grouped()
-            nc.scalar.copy(out=quad_view(grouped[:]), in_=z_read(0, n * COLS, (n + 1) * COLS))
-            z_grouped.append(grouped)
+        collect(0, 3, False)
+        layer1(1, 2)
         scatter(1, 2)
-        collect(1, 2)
-        layer1(1, 0)
-        cast_w2(1)
+        collect(1, 1, False)
+        layer1(1, 3)
         scatter(1, 3)
-        collect(1, 3)
-        quantize_w2(1)
+        collect(1, 2, False)
+        z_grouped = new_grouped(V, "z_grouped")
         for n in range(2):
-            quantize(z_q[0], n * COLS, z_grouped[n], 0, COLS)
-            layer2(0, n)
+            cast_part(nc.scalar.copy, z_grouped, z_read(0), n * COLS, (n + 1) * COLS)
+        quantize(z_q[0], 0, z_grouped, 0, V)
+        layer1(1, 0)
+        layer2(0, 0)
+        layer2(0, 1)
+        collect(1, 3, True)
         scatter(1, 0)
-        for v0 in (0, COLS):
-            nc.vector.tensor_copy(out=z_all[1][:, v0 : v0 + COLS], in_=z_plane[0][:, v0 : v0 + COLS])
 
-        near = new_grouped()
-        far = new_grouped()
-        nc.vector.tensor_copy(out=quad_view(near[:]), in_=z_read(1, 0, COLS))
-        nc.scalar.copy(out=quad_view(far[:]), in_=z_read(1, COLS, V))
+        z_last = z_read(1)
+        near = new_grouped(COLS, "x_a")
+        far = new_grouped(COLS, "x_b")
+        cast_part(nc.vector.tensor_copy, near, z_last[:, :, 0:COLS], 0, 320)
+        cast_part(nc.scalar.copy, near, z_last[:, :, 0:COLS], 320, COLS)
         quantize(z_q[1], 0, near, 0, COLS)
         layer2(1, 0)
+        cast_part(nc.vector.tensor_copy, far, z_last[:, :, COLS:V], 0, 192)
+        cast_part(nc.scalar.copy, far, z_last[:, :, COLS:V], 192, COLS)
         quantize(z_q[1], COLS, far, 0, COLS)
         layer2(1, 1)
         store(0)

@@ -8,6 +8,7 @@ F32 = mybir.dt.float32
 BF16 = mybir.dt.bfloat16
 U32 = mybir.dt.uint32
 U16 = mybir.dt.uint16
+I32 = mybir.dt.int32
 U8 = mybir.dt.uint8
 FP8X4 = mybir.dt.float8_e4m3fn_x4
 
@@ -20,7 +21,7 @@ K_PASS = P * PACK
 PASSES = 2
 COLS = 512
 
-X_CUT = (320, 320, 192, 256)
+X_CUT = (256, 256, 128, 256)
 
 FLOPS = 2 * K * S * H + 2 * H * V * N
 
@@ -65,8 +66,6 @@ def tile_picked_voxel_gelu_e_kernel(tc, xT, w1, w2, gate, offs, pos1, out):
         nc.gpsimd.memset(warm[:], 0.0)
         warmed = keep.tile([P, 2], F32, name="warmed")
         nc.scalar.activation(out=warmed[:], in_=warm[:], func=GELU)
-        first_bias = keep.tile([P, 1], F32, name="first_bias", tag="after_first_gelu", align_bytes=64)
-        nc.gpsimd.memset(first_bias[:], 0.0)
 
         all_bytes = keep.tile([P, T], U8, name="x_all_bytes", align_bytes=64)
         nc.gpsimd.memset(all_bytes[:], 0)
@@ -78,7 +77,7 @@ def tile_picked_voxel_gelu_e_kernel(tc, xT, w1, w2, gate, offs, pos1, out):
         z_all = []
         for g in range(PASSES):
             z_group = keep.tile([P, PACK * V], F32, name=f"z_all_{g}")
-            nc.gpsimd.memset(z_group[:, 0:V], 0.0)
+            nc.vector.memset(z_group[:, 0:V], 0.0)
             z_all.append(z_group)
         z_plane = {}
         for t in range(1, PACK):
@@ -117,16 +116,32 @@ def tile_picked_voxel_gelu_e_kernel(tc, xT, w1, w2, gate, offs, pos1, out):
         def cast_w1(engine_copy, g, s, t0, t1):
             if (g, s) not in w1_q:
                 w1_q[g, s] = new_operand(COLS, f"w1_{g}_{s}")
-            if (g, s) == (0, 1):
-                base, planes, slot = (0, 2, "w_01") if t0 < 2 else (2, 2, "after_first_gelu")
-            else:
-                base, planes, slot = 0, PACK, "w_b" if (g, s) == (1, 0) else "w_a"
+            base, planes = (0, PACK) if (g, s) == (0, 0) else ((0, 2) if t0 < 2 else (2, 2))
             if (g, s, base) not in w1_grouped:
-                grouped = new_grouped(planes * P, slot)
+                grouped = new_grouped(planes * P, f"w_0{s}_{base}")
                 w1_grouped[g, s, base] = grouped
             view = w1_grouped[g, s, base][:].rearrange("p (t m j) -> p m t j", t=planes, j=PACK)
             read = w1_raw[g, s][:].rearrange("p j (m t) -> p m t j", t=PACK)
-            engine_copy(out=view[:, :, t0 - base : t1 - base], in_=read[:, :, t0:t1])
+            engine_copy(view[:, :, t0 - base : t1 - base], read[:, :, t0:t1])
+
+        def gpsimd_cast(dest, source):
+            nc.gpsimd.tensor_scalar(dest, source, 1.0, 0.0, MULT, mybir.AluOpType.add)
+
+        late_grouped = []
+
+        def cast_late_w1(s):
+            if not late_grouped:
+                grouped = new_grouped(PASSES * COLS, "w_late")
+                late_grouped.append(grouped)
+            view = late_grouped[0][:].rearrange("p (s t m j) -> p s m t j", s=PASSES, t=PACK, j=PACK)
+            read = w1_raw[1, s][:].rearrange("p j (m t) -> p m t j", t=PACK)
+            nc.scalar.copy(out=view[:, s], in_=read)
+
+        def quantize_late_w1():
+            codes, scales = new_operand(PASSES * COLS, "w1_late")
+            quantize((codes, scales), 0, late_grouped[0], 0, PASSES * COLS)
+            for s in range(PASSES):
+                w1_q[1, s] = (codes[:, s * COLS : (s + 1) * COLS], scales[:, s * COLS : (s + 1) * COLS])
 
         def quantize_w1(g, s, t0, t1):
             base = 2 if (g, s) == (0, 1) and t0 >= 2 else 0
@@ -149,41 +164,52 @@ def tile_picked_voxel_gelu_e_kernel(tc, xT, w1, w2, gate, offs, pos1, out):
         nc.vector.tensor_copy(picked_bytes[:], all_bytes[:].indirect(idx[:]))
         x_bytes = [picked_bytes[4 * s : P, :] for s in range(PASSES)]
 
-        cast_w1(nc.scalar.copy, 0, 0, 0, PACK)
-        cast_w1(nc.scalar.copy, 0, 1, 0, 1)
+        cast_w1(nc.scalar.copy, 0, 0, 0, 2)
+        cast_w1(gpsimd_cast, 0, 0, 2, PACK)
         cast_w1(nc.scalar.copy, 0, 1, 1, 2)
+        cast_w1(nc.scalar.copy, 0, 1, 0, 1)
+        cast_w1(gpsimd_cast, 0, 1, 2, PACK)
         quantize_w1(0, 0, 0, PACK)
-        quantize_w1(0, 1, 0, 1)
+        quantize_w1(0, 1, 1, 2)
 
         hidden = {}
 
-        def layer1(g, t):
-            acc = psum.tile([P, S], F32, name="acc")
+        def layer1(g, t, pieces=1):
             cols = slice(t * P, (t + 1) * P)
-            for s in range(PASSES):
-                w_codes, w_scales = w1_q[g, s]
-                nc.tensor.matmul_mx(
-                    out=acc[:],
-                    lhsT=w_codes[:, cols].bitcast(FP8X4),
-                    lhsT_scale=w_scales[:, cols],
-                    rhs=x_words[s][:].bitcast(FP8X4),
-                    rhs_scale=x_bytes[s],
-                    start=(s == 0),
-                    stop=(s == PASSES - 1),
-                )
-            if (g, t) == (1, 0):
+            width = S // pieces
+            entries = [slice(i * width, (i + 1) * width) for i in range(pieces)]
+            accs = []
+            for picked in entries:
+                acc = psum.tile([P, width], F32, name="acc")
+                accs.append(acc)
+                for s in range(PASSES):
+                    w_codes, w_scales = w1_q[g, s]
+                    nc.tensor.matmul_mx(
+                        out=acc[:],
+                        lhsT=w_codes[:, cols].bitcast(FP8X4),
+                        lhsT_scale=w_scales[:, cols],
+                        rhs=x_words[s][:, picked].bitcast(FP8X4),
+                        rhs_scale=x_bytes[s][:, picked],
+                        start=(s == 0),
+                        stop=(s == PASSES - 1),
+                    )
+            if (g, t) in ((0, 2), (0, 3)):
+                h = keep.tile([P, S], F32, name="h_late", tag=f"w1_raw_1_{t - 2}")
+            elif (g, t) == (1, 0):
                 h = keep.tile([P, S], F32, name="h_last", tag="z_all_0")
             else:
                 h = ring.tile([P, S], F32, name="h")
-            if (g, t) == (0, 0):
-                nc.scalar.activation(out=h[:], in_=acc[:], func=GELU, bias=first_bias[:])
-            else:
-                nc.scalar.activation(out=h[:], in_=acc[:], func=GELU)
+            for acc, picked in zip(accs, entries):
+                nc.scalar.activation(out=h[:, picked], in_=acc[:], func=GELU)
             hidden[g, t] = h
 
-        def scatter(g, t):
+        def scatter(g, t, pieces=1):
             window = z_all[g] if t == 0 else z_plane[t]
-            nc.vector.tensor_tensor(window[:].indirect(cell[:]), hidden[g, t][:], gate_all[:], MULT)
+            width = S // pieces
+            for i in range(pieces):
+                part = slice(i * width, (i + 1) * width)
+                places = cell[:, i * width // 16 : (i + 1) * width // 16]
+                nc.vector.tensor_tensor(window[:].indirect(places), hidden[g, t][:, part], gate_all[:, part], MULT)
 
         def collect(g, t, last):
             region = z_all[g][:, t * V : (t + 1) * V]
@@ -200,10 +226,17 @@ def tile_picked_voxel_gelu_e_kernel(tc, xT, w1, w2, gate, offs, pos1, out):
 
         accs = {}
 
+        moved_codes = keep.tile([P, COLS], U32, name="moved_codes", align_bytes=64)
+
         def layer2(g, n):
             z_codes, z_scales = z_q[g]
             w_codes, w_scales = w2_q
             cols = slice(n * COLS, (n + 1) * COLS)
+            if (g, n) == (0, 1):
+                nc.sync.dma_start(out=moved_codes[:].bitcast(I32), in_=z_codes[:, cols].bitcast(I32))
+                moving = moved_codes[:]
+            else:
+                moving = z_codes[:, cols]
             for m in range(N // P):
                 if g == 0:
                     acc = psum.tile([P, COLS], F32, name="acc")
@@ -213,7 +246,7 @@ def tile_picked_voxel_gelu_e_kernel(tc, xT, w1, w2, gate, offs, pos1, out):
                     out=accs[m, n][:],
                     lhsT=w_codes[:, weights].bitcast(FP8X4),
                     lhsT_scale=w_scales[:, weights],
-                    rhs=z_codes[:, cols].bitcast(FP8X4),
+                    rhs=moving.bitcast(FP8X4),
                     rhs_scale=z_scales[:, cols],
                     start=(g == 0),
                     stop=(g == PASSES - 1),
@@ -228,20 +261,18 @@ def tile_picked_voxel_gelu_e_kernel(tc, xT, w1, w2, gate, offs, pos1, out):
                     nc.scalar.copy(out=result[:], in_=accs[m, n][:])
                 nc.sync.dma_start(out=out[m * P : (m + 1) * P, n * COLS : (n + 1) * COLS], in_=result[:])
 
-        layer1(0, 0)
-        quantize_w1(0, 1, 1, 2)
-        scatter(0, 0)
-        cast_w1(nc.scalar.copy, 0, 1, 2, PACK)
+        layer1(0, 1, pieces=2)
+        quantize_w1(0, 1, 0, 1)
         quantize_w1(0, 1, 2, PACK)
-        layer1(0, 1)
-        scatter(0, 1)
-        cast_w1(nc.scalar.copy, 1, 0, 0, PACK)
-        quantize_w1(1, 0, 0, PACK)
-        cast_w1(nc.scalar.copy, 1, 1, 0, PACK)
-        quantize_w1(1, 1, 0, PACK)
+        scatter(0, 1, pieces=2)
+        layer1(0, 0)
+        scatter(0, 0)
+        cast_late_w1(0)
         layer1(0, 2)
         scatter(0, 2)
         collect(0, 1, False)
+        cast_late_w1(1)
+        quantize_late_w1()
         layer1(0, 3)
         scatter(0, 3)
         collect(0, 2, False)
@@ -273,12 +304,12 @@ def tile_picked_voxel_gelu_e_kernel(tc, xT, w1, w2, gate, offs, pos1, out):
         z_last = z_read(1)
         near = new_grouped(COLS, "x_a")
         far = new_grouped(COLS, "x_b")
-        cast_part(nc.vector.tensor_copy, near, z_last[:, :, 0:COLS], 0, 320)
-        cast_part(nc.scalar.copy, near, z_last[:, :, 0:COLS], 320, COLS)
+        cast_part(nc.vector.tensor_copy, near, z_last[:, :, 0:COLS], 0, 352)
+        cast_part(nc.scalar.copy, near, z_last[:, :, 0:COLS], 352, COLS)
         quantize(z_q[1], 0, near, 0, COLS)
         layer2(1, 0)
-        cast_part(nc.vector.tensor_copy, far, z_last[:, :, COLS:V], 0, 192)
-        cast_part(nc.scalar.copy, far, z_last[:, :, COLS:V], 192, COLS)
+        cast_part(nc.vector.tensor_copy, far, z_last[:, :, COLS:V], 0, 208)
+        cast_part(nc.scalar.copy, far, z_last[:, :, COLS:V], 208, COLS)
         quantize(z_q[1], COLS, far, 0, COLS)
         layer2(1, 1)
         store(0)

from contextlib import ExitStack

import concourse.mybir as mybir

K, T, S, V, H, N = 1024, 1024, 512, 1024, 1024, 512

F32 = mybir.dt.float32
BF16 = mybir.dt.bfloat16
U32 = mybir.dt.uint32
U16 = mybir.dt.uint16
I32 = mybir.dt.int32
U8 = mybir.dt.uint8
FP8X4 = mybir.dt.float8_e4m3fn_x4

MULT = mybir.AluOpType.mult
GELU = mybir.ActivationFunctionType.Gelu_apprx_tanh

P = 128
PACK = 4
K_PASS = P * PACK
PASSES = 2
COLS = 512

X_CUT = (256, 256, 128, 256)

FLOPS = 2 * K * S * H + 2 * H * V * N


def tile_picked_voxel_gelu_e_kernel(tc, xT, w1, w2, gate, offs, pos1, out):
    nc = tc.nc
    with ExitStack() as ctx:
        lists = ctx.enter_context(tc.tile_pool(name="lists", bufs=1))
        keep = ctx.enter_context(tc.tile_pool(name="keep", bufs=1))
        ring = ctx.enter_context(tc.tile_pool(name="ring", bufs=5))
        psum = ctx.enter_context(tc.psum_pool(name="psum", bufs=8))

        idx = lists.tile([P, S // 16], U16, name="idx")
        cell = lists.tile([P, S // 16], U16, name="cell")
        nc.sync.dma_start(idx[:], offs)

        def load_rows(source, name):
            raw = keep.tile([P, PACK, COLS], F32, name=name)
            nc.sync.dma_start(out=raw[:], in_=source.rearrange("(p j) c -> p j c", j=PACK))
            return raw

        def rows(k):
            return slice(k * K_PASS, (k + 1) * K_PASS)

        x_raw = {}
        for s in range(PASSES):
            for c in range(2):
                x_raw[s, c] = load_rows(xT[rows(s), c * COLS : (c + 1) * COLS], f"x_raw_{s}_{c}")
        w1_raw = {}
        for s in range(PASSES):
            w1_raw[0, s] = load_rows(w1[rows(s), 0:COLS], f"w1_raw_0_{s}")
        nc.sync.dma_start(cell[:], pos1)
        gate_all = keep.tile([P, S], F32, name="gate_all")
        nc.sync.dma_start(out=gate_all[:], in_=gate)
        for s in range(PASSES):
            w1_raw[1, s] = load_rows(w1[rows(s), COLS : 2 * COLS], f"w1_raw_1_{s}")
        w2_raw = []
        for g in range(PASSES):
            w2_raw.append(load_rows(w2[rows(g), :], f"w2_raw_{g}"))

        warm = keep.tile([P, 2], F32, name="warm")
        nc.gpsimd.memset(warm[:], 0.0)
        warmed = keep.tile([P, 2], F32, name="warmed")
        nc.scalar.activation(out=warmed[:], in_=warm[:], func=GELU)

        all_bytes = keep.tile([P, T], U8, name="x_all_bytes", align_bytes=64)
        nc.gpsimd.memset(all_bytes[:], 0)
        x_all = []
        for s in range(PASSES):
            words = keep.tile([P, T], U32, name=f"x_all_words_{s}", align_bytes=64)
            x_all.append((words, all_bytes[4 * s : P, :]))

        z_all = []
        for g in range(PASSES):
            z_group = keep.tile([P, PACK * V], F32, name=f"z_all_{g}")
            nc.vector.memset(z_group[:, 0:V], 0.0)
            z_all.append(z_group)
        z_plane = {}
        for t in range(1, PACK):
            plane = keep.tile([P, V], F32, name=f"z_plane_{t}")
            nc.gpsimd.memset(plane[:], 0.0)
            z_plane[t] = plane

        def new_operand(cols, name):
            codes = keep.tile([P, cols], U32, name=name + "_codes", align_bytes=64)
            scales = keep.tile([P, cols], U8, name=name + "_scales", align_bytes=64)
            return codes, scales

        def quantize(operand, c0, grouped, g0, width):
            codes, scales = operand
            nc.vector.quantize_mx(
                out=codes[:, c0 : c0 + width].bitcast(FP8X4),
                scales=scales[:, c0 : c0 + width],
                in_=grouped[:, PACK * g0 : PACK * (g0 + width)],
            )

        def new_grouped(cols, slot):
            return keep.tile([P, PACK * cols], BF16, name="grouped", tag=slot, align_bytes=64)

        def quad_view(grouped_cols):
            return grouped_cols.rearrange("p (c i t) -> p c t i", i=4, t=PACK)

        def quad_read(source):
            return source.rearrange("p t (c i) -> p c t i", i=4)

        def cast_part(engine_copy, grouped, source, c0, c1):
            engine_copy(out=quad_view(grouped[:, PACK * c0 : PACK * c1]), in_=quad_read(source[:, :, c0:c1]))

        w1_q = {}
        w1_grouped = {}

        def cast_w1(engine_copy, g, s, t0, t1):
            if (g, s) not in w1_q:
                w1_q[g, s] = new_operand(COLS, f"w1_{g}_{s}")
            base, planes = (0, PACK) if (g, s) == (0, 0) else ((0, 2) if t0 < 2 else (2, 2))
            if (g, s, base) not in w1_grouped:
                grouped = new_grouped(planes * P, f"w_0{s}_{base}")
                w1_grouped[g, s, base] = grouped
            view = w1_grouped[g, s, base][:].rearrange("p (t m j) -> p m t j", t=planes, j=PACK)
            read = w1_raw[g, s][:].rearrange("p j (m t) -> p m t j", t=PACK)
            engine_copy(view[:, :, t0 - base : t1 - base], read[:, :, t0:t1])

        def gpsimd_cast(dest, source):
            nc.gpsimd.tensor_scalar(dest, source, 1.0, 0.0, MULT, mybir.AluOpType.add)

        late_grouped = []

        def cast_late_w1(s):
            if not late_grouped:
                grouped = new_grouped(PASSES * COLS, "w_late")
                late_grouped.append(grouped)
            view = late_grouped[0][:].rearrange("p (s t m j) -> p s m t j", s=PASSES, t=PACK, j=PACK)
            read = w1_raw[1, s][:].rearrange("p j (m t) -> p m t j", t=PACK)
            nc.scalar.copy(out=view[:, s], in_=read)

        def quantize_late_w1():
            codes, scales = new_operand(PASSES * COLS, "w1_late")
            quantize((codes, scales), 0, late_grouped[0], 0, PASSES * COLS)
            for s in range(PASSES):
                w1_q[1, s] = (codes[:, s * COLS : (s + 1) * COLS], scales[:, s * COLS : (s + 1) * COLS])

        def quantize_w1(g, s, t0, t1):
            base = 2 if (g, s) == (0, 1) and t0 >= 2 else 0
            quantize(w1_q[g, s], t0 * P, w1_grouped[g, s, base], (t0 - base) * P, (t1 - t0) * P)

        x_words = []
        x_bytes = []
        for s in range(PASSES):
            for c in range(2):
                grouped = new_grouped(COLS, "x_a" if c == 0 else "x_b")
                cut = X_CUT[2 * s + c]
                if cut:
                    cast_part(nc.vector.tensor_copy, grouped, x_raw[s, c], 0, cut)
                cast_part(nc.scalar.copy, grouped, x_raw[s, c], cut, COLS)
                quantize(x_all[s], c * COLS, grouped, 0, COLS)
            words = keep.tile([P, S], U32, name=f"x_words_{s}", align_bytes=64)
            nc.vector.tensor_copy(words[:], x_all[s][0][:].indirect(idx[:]))
            x_words.append(words)
        picked_bytes = keep.tile([P, S], U8, name="x_bytes", align_bytes=64)
        nc.vector.tensor_copy(picked_bytes[:], all_bytes[:].indirect(idx[:]))
        x_bytes = [picked_bytes[4 * s : P, :] for s in range(PASSES)]

        cast_w1(nc.scalar.copy, 0, 0, 0, 2)
        cast_w1(gpsimd_cast, 0, 0, 2, PACK)
        cast_w1(nc.scalar.copy, 0, 1, 1, 2)
        cast_w1(nc.scalar.copy, 0, 1, 0, 1)
        cast_w1(gpsimd_cast, 0, 1, 2, PACK)
        quantize_w1(0, 0, 0, PACK)
        quantize_w1(0, 1, 1, 2)

        hidden = {}

        def layer1(g, t, pieces=1):
            cols = slice(t * P, (t + 1) * P)
            width = S // pieces
            entries = [slice(i * width, (i + 1) * width) for i in range(pieces)]
            accs = []
            for picked in entries:
                acc = psum.tile([P, width], F32, name="acc")
                accs.append(acc)
                for s in range(PASSES):
                    w_codes, w_scales = w1_q[g, s]
                    nc.tensor.matmul_mx(
                        out=acc[:],
                        lhsT=w_codes[:, cols].bitcast(FP8X4),
                        lhsT_scale=w_scales[:, cols],
                        rhs=x_words[s][:, picked].bitcast(FP8X4),
                        rhs_scale=x_bytes[s][:, picked],
                        start=(s == 0),
                        stop=(s == PASSES - 1),
                    )
            if (g, t) in ((0, 2), (0, 3)):
                h = keep.tile([P, S], F32, name="h_late", tag=f"w1_raw_1_{t - 2}")
            elif (g, t) == (1, 0):
                h = keep.tile([P, S], F32, name="h_last", tag="z_all_0")
            else:
                h = ring.tile([P, S], F32, name="h")
            for acc, picked in zip(accs, entries):
                nc.scalar.activation(out=h[:, picked], in_=acc[:], func=GELU)
            hidden[g, t] = h

        def scatter(g, t, pieces=1):
            window = z_all[g] if t == 0 else z_plane[t]
            width = S // pieces
            for i in range(pieces):
                part = slice(i * width, (i + 1) * width)
                places = cell[:, i * width // 16 : (i + 1) * width // 16]
                nc.vector.tensor_tensor(window[:].indirect(places), hidden[g, t][:, part], gate_all[:, part], MULT)

        def collect(g, t, last):
            region = z_all[g][:, t * V : (t + 1) * V]
            if last:
                nc.scalar.copy(out=region, in_=z_plane[t][:])
            else:
                nc.sync.dma_start(out=region, in_=z_plane[t][:])

        w2_q = new_operand(PASSES * N, "w2")
        z_q = [new_operand(V, f"z_{g}") for g in range(PASSES)]

        def z_read(g):
            return z_all[g][:].rearrange("p (t v) -> p t v", t=PACK)

        accs = {}

        moved_codes = keep.tile([P, COLS], U32, name="moved_codes", align_bytes=64)

        def layer2(g, n):
            z_codes, z_scales = z_q[g]
            w_codes, w_scales = w2_q
            cols = slice(n * COLS, (n + 1) * COLS)
            if (g, n) == (0, 1):
                nc.sync.dma_start(out=moved_codes[:].bitcast(I32), in_=z_codes[:, cols].bitcast(I32))
                moving = moved_codes[:]
            else:
                moving = z_codes[:, cols]
            for m in range(N // P):
                if g == 0:
                    acc = psum.tile([P, COLS], F32, name="acc")
                    accs[m, n] = acc
                weights = slice(g * N + m * P, g * N + (m + 1) * P)
                nc.tensor.matmul_mx(
                    out=accs[m, n][:],
                    lhsT=w_codes[:, weights].bitcast(FP8X4),
                    lhsT_scale=w_scales[:, weights],
                    rhs=moving.bitcast(FP8X4),
                    rhs_scale=z_scales[:, cols],
                    start=(g == 0),
                    stop=(g == PASSES - 1),
                )

        def store(n):
            for m in range(N // P):
                result = keep.tile([P, COLS], F32, name=f"result_{m}_{n}")
                if m % 2 == 0:
                    nc.vector.tensor_copy(out=result[:], in_=accs[m, n][:])
                else:
                    nc.scalar.copy(out=result[:], in_=accs[m, n][:])
                nc.sync.dma_start(out=out[m * P : (m + 1) * P, n * COLS : (n + 1) * COLS], in_=result[:])

        layer1(0, 1, pieces=2)
        quantize_w1(0, 1, 0, 1)
        quantize_w1(0, 1, 2, PACK)
        scatter(0, 1, pieces=2)
        layer1(0, 0)
        scatter(0, 0)
        cast_late_w1(0)
        layer1(0, 2)
        scatter(0, 2)
        collect(0, 1, False)
        cast_late_w1(1)
        quantize_late_w1()
        layer1(0, 3)
        scatter(0, 3)
        collect(0, 2, False)
        layer1(1, 1)
        w2_grouped = new_grouped(PASSES * N, "w2_grouped")
        for g in range(PASSES):
            nc.scalar.copy(
                out=quad_view(w2_grouped[:, g * PACK * N : (g + 1) * PACK * N]), in_=quad_read(w2_raw[g][:])
            )
        quantize(w2_q, 0, w2_grouped, 0, PASSES * N)
        scatter(1, 1)
        collect(0, 3, False)
        layer1(1, 2)
        scatter(1, 2)
        collect(1, 1, False)
        layer1(1, 3)
        scatter(1, 3)
        collect(1, 2, False)
        z_grouped = new_grouped(V, "z_grouped")
        for n in range(2):
            cast_part(nc.scalar.copy, z_grouped, z_read(0), n * COLS, (n + 1) * COLS)
        quantize(z_q[0], 0, z_grouped, 0, V)
        layer1(1, 0)
        layer2(0, 0)
        layer2(0, 1)
        collect(1, 3, True)
        scatter(1, 0)

        z_last = z_read(1)
        near = new_grouped(COLS, "x_a")
        far = new_grouped(COLS, "x_b")
        cast_part(nc.vector.tensor_copy, near, z_last[:, :, 0:COLS], 0, 352)
        cast_part(nc.scalar.copy, near, z_last[:, :, 0:COLS], 352, COLS)
        quantize(z_q[1], 0, near, 0, COLS)
        layer2(1, 0)
        cast_part(nc.vector.tensor_copy, far, z_last[:, :, COLS:V], 0, 208)
        cast_part(nc.scalar.copy, far, z_last[:, :, COLS:V], 208, COLS)
        quantize(z_q[1], COLS, far, 0, COLS)
        layer2(1, 1)
        store(0)
        store(1)
